import numpy as np
import ml_dtypes


def mxq(x, axis, fmt="e4m3"):
    dtype, down = {"e4m3": (ml_dtypes.float8_e4m3fn, 7), "e5m2": (ml_dtypes.float8_e5m2, 14)}[fmt]
    v = np.moveaxis(np.asarray(x, np.float32).astype(ml_dtypes.bfloat16).astype(np.float64), axis, -1)
    blocks = v.reshape(v.shape[:-1] + (-1, 32))
    amax = np.abs(blocks).max(-1, keepdims=True)
    byte = np.maximum(np.where(amax > 0, np.frexp(amax)[1] - 1 + 127, 0) - down, 1)
    scale = np.exp2(byte - 127.0)
    codes = (blocks / scale).astype(np.float32).astype(dtype).astype(np.float64)
    return np.moveaxis((codes * scale).reshape(v.shape), -1, axis)


WIDE = False


def mx_kscale(k):
    if not WIDE:
        return np.ones(k)
    levels = np.array([10, -10, 5, -5, 0])
    if k % 512:
        return np.exp2(np.random.permutation(np.resize(levels, k // 32))).repeat(32)
    a = np.empty((k // 512, 16))
    for p in range(k // 512):
        a[p, :8] = np.random.permutation(np.resize(levels, 8))
        for g in range(8):
            far = levels[np.abs(levels - a[p, g]) >= 10]
            a[p, g + 8] = far[np.random.randint(len(far))]
    return np.exp2(a.ravel()).repeat(32)


BF16 = ml_dtypes.bfloat16


def bf(x):
    return np.asarray(x, np.float32).astype(BF16)


def f64(x):
    return np.asarray(x).astype(np.float64)


E2M1 = np.array([0.0, 0.5, 1.0, 1.5, 2.0, 3.0, 4.0, 6.0, -0.0, -0.5, -1.0, -1.5, -2.0, -3.0, -4.0, -6.0])


def pack_weight(w, fmt):
    k, n = w.shape
    w = f64(bf(w)).reshape(k // 32, 32, n)
    amax = np.abs(w).max(1)
    if fmt == "e4m3":
        byte = np.frexp(amax)[1] - 1 + 127 - 7
    else:
        mant, ex = np.frexp(amax / 6.0)
        byte = np.where(mant > 0.5, ex, ex - 1) + 127
    byte = np.clip(np.where(amax > 0, byte, 1), 1, 254)
    scaled = (w * np.exp2(127.0 - byte)[:, None, :]).reshape(k, n).astype(np.float32)
    by_word = np.ascontiguousarray(scaled.reshape(k // 512, 128, 4, n).transpose(0, 1, 3, 2))
    if fmt == "e4m3":
        words = by_word.astype(ml_dtypes.float8_e4m3fn).view(np.uint8)
    else:
        c = by_word.astype(ml_dtypes.float4_e2m1fn).view(np.uint8) & 0xF
        words = c[..., 0::2] | (c[..., 1::2] << 4)
    return np.ascontiguousarray(words), np.ascontiguousarray(byte.astype(np.uint8).reshape(k // 512, 16, n))


def unpack_weight(words, scales, fmt):
    g, p, n, _ = words.shape
    if fmt == "e4m3":
        vals = np.ascontiguousarray(words).view(ml_dtypes.float8_e4m3fn).astype(np.float64)
    else:
        nib = np.empty((g, p, n, 4), np.uint8)
        nib[..., 0::2] = words & 0xF
        nib[..., 1::2] = words >> 4
        vals = E2M1[nib]
    vals = vals * np.repeat(np.exp2(scales.astype(np.float64) - 127.0), 8, axis=1)[..., None]
    return vals.transpose(0, 1, 3, 2).reshape(g * 512, n)
def pack4(w):
    words, scales = pack_weight(w, "e2m1")
    return words.reshape(words.shape[0], 128, -1), scales


def unpack4(words, scales):
    return unpack_weight(words.reshape(words.shape[0], 128, -1, 2), scales, "e2m1")


M, K, Q, R = 1024, 1024, 1536, 512

ETA_INF = 0.1
POWER = -0.3


def draw0():
    s, t, v = mx_kscale(K), mx_kscale(Q), mx_kscale(Q)
    u = np.random.standard_normal((M, K))
    bx_words, bx_scales = pack4(np.random.standard_normal((K, Q)) / np.sqrt(K) / s[:, None])
    by_words, by_scales = pack4(np.random.standard_normal((K, Q)) / np.sqrt(K) / s[:, None])
    px_words, px_scales = pack4(np.random.standard_normal((Q, R)) / np.sqrt(Q) / t[:, None])
    py_words, py_scales = pack4(np.random.standard_normal((Q, R)) / np.sqrt(Q) / v[:, None])
    return {"u": bf(u * s),
            "bx_words": bx_words, "bx_scales": bx_scales,
            "by_words": by_words, "by_scales": by_scales,
            "lift_x": bf(0.4 * np.random.standard_normal(Q)),
            "lift_y": bf(0.4 * np.random.standard_normal(Q)),
            "lam": bf(0.5 + np.random.random(Q)),
            "kxx": bf((1.2 + 0.2 * np.random.standard_normal(Q)) * t),
            "kxy": bf((0.4 + 0.2 * np.random.standard_normal(Q)) * t),
            "kyx": bf((-0.4 + 0.2 * np.random.standard_normal(Q)) * v),
            "kyy": bf((1.2 + 0.2 * np.random.standard_normal(Q)) * v),
            "px_words": px_words, "px_scales": px_scales,
            "py_words": py_words, "py_scales": py_scales,
            "load": bf(0.4 * np.random.standard_normal(R))}


def core(u, bx_words, bx_scales, by_words, by_scales, lift_x, lift_y, lam,
              kxx, kxy, kyx, kyy, px_words, px_scales, py_words, py_scales, load):
    uq = mxq(f64(u), 1, "e4m3")
    hx = (uq @ unpack4(bx_words, bx_scales)) + f64(lift_x)
    hy = (uq @ unpack4(by_words, by_scales)) + f64(lift_y)
    eta = ETA_INF + (1.0 - ETA_INF) * (1.0 + f64(lam) * (hx * hx + hy * hy)) ** POWER
    fx = eta * (f64(kxx) * hx + f64(kxy) * hy)
    fy = eta * (f64(kyx) * hx + f64(kyy) * hy)
    rx = mxq(fx, 1, "e4m3") @ unpack4(px_words, px_scales)
    ry = mxq(fy, 1, "e4m3") @ unpack4(py_words, py_scales)
    return rx + ry - f64(load)


def e4m3fn_bytes(y):
    return np.clip(np.asarray(y, np.float64), -448.0, 448.0).astype(np.float32).astype(ml_dtypes.float8_e4m3fn).view(np.uint8)


def e4m3fn_values(b):
    return np.asarray(b, np.uint8).view(ml_dtypes.float8_e4m3fn).astype(np.float64)


def setup_inputs():
    d = draw0()
    x0 = np.asarray(d['u']).astype(np.float64)
    s = (np.max(np.abs(x0), axis=(0,), keepdims=True) / 448.0).astype(np.float32)
    out = {}
    for k, v in d.items():
        if k == 'u':
            out['u_bytes'] = e4m3fn_bytes(x0 / s.astype(np.float64))
            out['u_scale'] = s
        else:
            out[k] = v
    return out


def reference(u_bytes, u_scale, bx_words, bx_scales, by_words, by_scales, lift_x, lift_y, lam, kxx, kxy, kyx, kyy, px_words, px_scales, py_words, py_scales, load):
    return core(e4m3fn_values(u_bytes) * u_scale.astype(np.float64), bx_words, bx_scales, by_words, by_scales, lift_x, lift_y, lam, kxx, kxy, kyx, kyy, px_words, px_scales, py_words, py_scales, load)

@@ -1,0 +1,480 @@
+from contextlib import ExitStack
+
+import concourse.mybir as mybir
+from concourse.masks import make_identity
+
+M, K, Q, R = 1024, 1024, 1536, 512
+FLOPS = 2 * M * K * 2 * Q + 2 * M * Q * 2 * R
+
+F32 = mybir.dt.float32
+BF16 = mybir.dt.bfloat16
+I32 = mybir.dt.int32
+U32 = mybir.dt.uint32
+U8 = mybir.dt.uint8
+FP8 = mybir.dt.float8_e4m3fn
+FP8X4 = mybir.dt.float8_e4m3fn_x4
+FP4X4 = mybir.dt.float4_e2m1fn_x4
+ALU = mybir.AluOpType
+ACT = mybir.ActivationFunctionType
+
+P = 128
+H = 512
+KG = K // 512
+QG = Q // 512
+BANKS = {"px": 2, "py": 3, "ss": 2, "acc": 1}
+UNITS = [(0, 0), (0, 1), (0, 2), (1, 0), (1, 1), (1, 2)]
+BATCHES = [[(0, 0, 512), (1, 0, 512), (2, 0, 512)], [(3, 0, 512), (4, 0, 512)], [(5, 0, 512)]]
+MODE = "GGGGGGGGGGGGGGGGGGGGGGGGGGGGGG"
+SADD_ON_V = {1, 3, 5, 7, 9, 11, 13, 21}
+EXPS = 2
+BURST = [0, 0]
+LAG2 = [0, 0]
+OUTS = [7, 8, 9, 10]
+UPREP = [2, 3, 6, 7]
+PS = [1, 5]
+UPT = [5, 6, 8, 9]
+SPLIT = 0
+GLAG = 1
+LNLAG = 1
+
+
+def tile_carreau_galerkin_residual_f1_kernel(
+    tc, u_bytes, u_scale, bx_words, bx_scales, by_words, by_scales, lift_x, lift_y, lam,
+    kxx, kxy, kyx, kyy, px_words, px_scales, py_words, py_scales, load, out
+):
+    nc = tc.nc
+    with ExitStack() as ctx:
+        keep = ctx.enter_context(tc.tile_pool(name="keep", bufs=1))
+        work = ctx.enter_context(tc.tile_pool(name="work", bufs=2))
+        psum = ctx.enter_context(tc.psum_pool(name="psum", bufs=2))
+        ctx.enter_context(tc.manual_schedule(engines={mybir.EngineType.Activation}))
+
+        scale_bc = keep.tile([P, K], F32, name="scale_bc", align_bytes=64)
+        load_bc = keep.tile([P, R], BF16, name="load_bc", align_bytes=64)
+        uq = keep.tile([P, KG, M], U32, name="uq", align_bytes=64)
+        uqs = keep.tile([P, KG, M], U8, name="uqs", align_bytes=64)
+        raws = keep.tile([P, 2, KG, Q], U8, name="raws", align_bytes=64)
+        perms = keep.tile([P, QG, 2 * KG, 4, P], U8, name="perms", align_bytes=64)
+        permw = keep.tile([P, QG, 4, 2 * KG, 2 * P], U8, name="permw", align_bytes=64)
+        pw = keep.tile([P, 2, QG, 2 * R], U8, name="pw", align_bytes=64)
+        psc = keep.tile([P, 2, QG, R], U8, name="psc", align_bytes=64)
+        vrow = keep.tile([P, 512], BF16, name="vrow", align_bytes=64)
+        vecs = keep.tile([P, 4, 21], F32, name="vecs", align_bytes=64)
+        k9 = keep.tile([P, 4, 12], F32, name="k9", align_bytes=64)
+        cc = keep.tile([P, 4, 6], F32, name="cc", align_bytes=64)
+        cm = keep.tile([P, 4, 6], F32, name="cm", align_bytes=64)
+        dummy = keep.tile([P, 2], F32, name="dummy", align_bytes=64)
+        ident = keep.tile([P, P], F32, name="ident", align_bytes=64)
+        identb = keep.tile([P, P], BF16, name="identb", align_bytes=64)
+
+        ub = []
+        for h in range(2):
+            ubh = work.tile([P, 4, K], U8, name="ubh", tag="ubh", bufs=2, align_bytes=64)
+            ub.append(ubh)
+        rawws = []
+        nc.vector.memset(raws[:].rearrange("p a k n -> p (a k n)").bitcast(I32), 0)
+        nc.sync.dma_start(out=scale_bc[:], in_=u_scale.rearrange("o k -> (o k)").partition_broadcast(P))
+        for r in range(4):
+            nc.sync.dma_start(out=ub[0][:, r, :], in_=u_bytes[r * P:(r + 1) * P, :])
+
+        def load_raww(g):
+            rw = work.tile([P, 2, KG, 1024], U8, name="rw", tag="rw", bufs=2, align_bytes=64)
+            for a, w in ((0, bx_words), (1, by_words)):
+                nc.sync.dma_start(out=rw[:, a, :, :], in_=w[:, :, g * 1024:(g + 1) * 1024].rearrange("k p c -> p k c"))
+            rawws.append(rw)
+
+        for a, s in ((0, bx_scales), (1, by_scales)):
+            for q4 in range(4):
+                nc.sync.dma_start(
+                    out=raws[32 * q4:32 * q4 + 4, a, :, :].bitcast(I32),
+                    in_=s[:, 4 * q4:4 * q4 + 4, :].rearrange("k r n -> r k n").bitcast(I32))
+        load_raww(0)
+        nc.gpsimd.memset(vrow[:], 0.0)
+        nc.gpsimd.memset(dummy[:], 1.0)
+        make_identity(nc, ident[:])
+        make_identity(nc, identb[:])
+        nc.gpsimd.memset(psc[:].rearrange("p a g n -> p (a g n)").bitcast(I32), 0)
+        for v, vec in enumerate((lift_x, lift_y, lam, kxx, kxy, kyx, kyy)):
+            nc.scalar.dma_start(out=vrow[3 * v:3 * v + 3, :], in_=vec.rearrange("(g n) -> g n", g=QG))
+        nc.scalar.activation(out=dummy[:, 1:2], in_=dummy[:, 0:1], func=ACT.Ln)
+        nc.sync.dma_start(out=ub[1][:], in_=u_bytes[H:2 * H, :].rearrange("(r p) k -> p r k", p=P))
+        load_raww(1)
+        nc.scalar.dma_start(out=load_bc[:], in_=load.partition_broadcast(P))
+
+        def late_loads():
+            load_raww(2)
+            for a, w in ((0, px_words), (1, py_words)):
+                nc.sync.dma_start(out=pw[:, a, :, :], in_=w.rearrange("g p c -> p g c"))
+            for a, s in ((0, px_scales), (1, py_scales)):
+                for q4 in range(4):
+                    nc.sync.dma_start(
+                        out=psc[32 * q4:32 * q4 + 4, a, :, :].bitcast(I32),
+                        in_=s[:, 4 * q4:4 * q4 + 4, :].rearrange("g r n -> r g n").bitcast(I32))
+
+        def bank(tag):
+            t = psum.tile([P, 512], F32, name="ps_" + tag, tag=tag, bufs=BANKS[tag])
+            return t
+
+        ubf = {}
+        uT = {}
+        tp = {}
+
+        def product(h, r):
+            t = work.tile([P, K], BF16, name="ubf", tag="ubf", bufs=2, align_bytes=64)
+            nc.vector.tensor_tensor(out=t[:], in0=ub[h][:, r, :].bitcast(FP8), in1=scale_bc[:], op=ALU.mult)
+            ubf[(h, r)] = t
+
+        def transposes(h, r, tags):
+            words = ubf[(h, r)][:].bitcast(F32)
+            for g in range(KG):
+                if r % 2 == 0:
+                    tp[(h, r // 2, g)] = bank(tags[g])
+                b = tp[(h, r // 2, g)]
+                for w in range(2):
+                    c0 = (r % 2) * 256 + w * 128
+                    nc.tensor.transpose(b[:, c0:c0 + 128], words[:, 256 * g + w:256 * (g + 1):2], ident[:])
+
+        def tcopy(h, rp, g, eng):
+            if rp == 0:
+                uT[(h, g)] = work.tile([P, 4 * H], BF16, name="uT", tag="uT", bufs=2, align_bytes=64)
+            o = uT[(h, g)][:].bitcast(F32)[:, rp * 512:(rp + 1) * 512].rearrange("p (s n w) -> p s n w", s=2, w=2)
+            i = tp[(h, rp, g)][:].rearrange("p (s w n) -> p s n w", s=2, w=2)
+            eng(o, i)
+
+        def scopy(o, i):
+            nc.scalar.copy(out=o, in_=i)
+
+        def vcopy(o, i):
+            nc.vector.tensor_copy(out=o, in_=i)
+
+        def uquant(h, g, m0, m1):
+            n = slice(h * H + m0, h * H + m1)
+            nc.vector.quantize_mx(out=uq[:, g, n].bitcast(FP8X4), scales=uqs[:, g, n],
+                                  in_=uT[(h, g)][:, 4 * m0:4 * m1])
+
+        def perm_scales(g):
+            for a in range(2):
+                nc.vector.tensor_copy(
+                    out=perms[:, g, a * KG:(a + 1) * KG, :, :],
+                    in_=raws[:, a, :, g * 512:(g + 1) * 512].rearrange("p k (m t) -> p k t m", t=4))
+
+        def perm_words(g, t):
+            nc.vector.tensor_copy(
+                out=permw[:, g, t, :, :].rearrange("p k (m b) -> p k m b", b=2),
+                in_=rawws[g][:].rearrange("p a k (m t b) -> p (a k) t m b", t=4, b=2)[:, :, t, :, :])
+
+        tiles = []
+        batch_end = {}
+        for b in BATCHES:
+            for ui, m0, m1 in b:
+                h, g = UNITS[ui]
+                for t in range(4):
+                    ms = [(m0, m1)]
+                    if ui == 0 and t < SPLIT:
+                        ms = [(m0, 256), (256, m1)]
+                    for a0, a1 in ms:
+                        tiles.append((h, g, t, ui, a0, a1))
+            batch_end[len(tiles) - 1] = b
+        NT = len(tiles)
+        last = NT - 1
+        first_h1 = [n for n in range(NT) if tiles[n][0] == 1][0]
+        px, py, ss, sq, tt = {}, {}, {}, {}, {}
+        gX, gY, E, FX, FY = {}, {}, {}, {}, {}
+        fq = {}
+
+        def stage1(i):
+            h, g, t, ui, m0, m1 = tiles[i]
+            w = m1 - m0
+            px[i], py[i] = bank("px"), bank("py")
+            step = 512 if w == 512 else 128
+            for a, b in ((1, py[i]), (0, px[i])):
+                for c in range(0, w, step):
+                    n0 = h * H + m0 + c
+                    for k in range(KG):
+                        nc.tensor.matmul_mx(
+                            out=b[:, c:c + step], lhsT=permw[:, g, t, a * KG + k, :].bitcast(FP4X4),
+                            lhsT_scale=perms[:, g, a * KG + k, t, :],
+                            rhs=uq[:, k, n0:n0 + step].bitcast(FP8X4),
+                            rhs_scale=uqs[:, k, n0:n0 + step], start=(k == 0), stop=(k == KG - 1))
+
+        def col(v, g, t):
+            return vecs[:, t, 3 * v + g:3 * v + g + 1]
+
+        def squares(i):
+            h, g, t, ui, m0, m1 = tiles[i]
+            w = m1 - m0
+            hy2 = work.tile([P, H], F32, name="hy2", tag="hy2", bufs=2, align_bytes=64)
+            nc.scalar.activation(out=hy2[:, :w], in_=py[i][:, :w], func=ACT.Square, bias=col(1, g, t))
+            hx2 = work.tile([P, H], F32, name="hx2", tag="hx2", bufs=2, align_bytes=64)
+            if MODE[i] == "G":
+                hx = work.tile([P, H], F32, name="hx", tag="hx", bufs=2, align_bytes=64)
+                nc.scalar.activation(out=hx[:, :w], in_=px[i][:, :w], func=ACT.Identity, bias=col(0, g, t))
+                nc.scalar.activation(out=hx2[:, :w], in_=hx[:, :w], func=ACT.Square)
+                for a in range(2):
+                    tx = work.tile([P, H], F32, name="t" + "xy"[a], tag="t" + "xy"[a], bufs=2, align_bytes=64)
+                    nc.gpsimd.tensor_scalar(out=tx[:, :w], in0=hx[:, :w], scalar1=k9[:, t, 6 * a + g:6 * a + g + 1],
+                                            scalar2=cm[:, t, 3 * a + g:3 * a + g + 1], op0=ALU.mult, op1=ALU.add)
+                    tt[(i, a)] = tx
+            else:
+                nc.scalar.activation(out=hx2[:, :w], in_=px[i][:, :w], func=ACT.Square, bias=col(0, g, t))
+            sq[i] = (hx2, hy2)
+
+        def t1(i):
+            h, g, t, ui, m0, m1 = tiles[i]
+            w = m1 - m0
+            tx = work.tile([P, H], F32, name="tx", tag="tx", bufs=2, align_bytes=64)
+            nc.scalar.activation(out=tx[:, :w], in_=px[i][:, :w], func=ACT.Identity, scale=k9[:, t, g:g + 1], bias=cc[:, t, g:g + 1])
+            tt[(i, 0)] = tx
+
+        def t2(i, on_v):
+            h, g, t, ui, m0, m1 = tiles[i]
+            w = m1 - m0
+            ty = work.tile([P, H], F32, name="ty", tag="ty", bufs=2, align_bytes=64)
+            if on_v:
+                nc.vector.tensor_scalar(out=ty[:, :w], in0=px[i][:, :w], scalar1=k9[:, t, 6 + g:7 + g],
+                                        scalar2=cc[:, t, 3 + g:4 + g], op0=ALU.mult, op1=ALU.add)
+            else:
+                nc.scalar.activation(out=ty[:, :w], in_=px[i][:, :w], func=ACT.Identity, scale=k9[:, t, 6 + g:7 + g],
+                                     bias=cc[:, t, 3 + g:4 + g])
+            tt[(i, 1)] = ty
+
+        def gradients(i):
+            h, g, t, ui, m0, m1 = tiles[i]
+            w = m1 - m0
+            if ui not in gX:
+                gX[ui] = work.tile([P, 4, H], F32, name="gx", tag="gx", bufs=4, align_bytes=64)
+                gY[ui] = work.tile([P, 4, H], F32, name="gy", tag="gy", bufs=4, align_bytes=64)
+            for a, dst in ((0, gX[ui]), (1, gY[ui])):
+                kc = 3 + g if a == 0 else 9 + g
+                nc.vector.scalar_tensor_tensor(out=dst[:, t, m0:m1], in0=py[i][:, :w], scalar=k9[:, t, kc:kc + 1],
+                                               in1=tt[(i, a)][:, :w], op0=ALU.mult, op1=ALU.add)
+
+        def sadd(i):
+            h, g, t, ui, m0, m1 = tiles[i]
+            w = m1 - m0
+            hx2, hy2 = sq[i]
+            if i in SADD_ON_V:
+                sv = work.tile([P, H], F32, name="sv", tag="sv", bufs=3, align_bytes=64)
+                ss[i] = sv
+                nc.vector.tensor_tensor(out=sv[:, :w], in0=hx2[:, :w], in1=hy2[:, :w], op=ALU.add)
+                return
+            ss[i] = bank("ss")
+            nc.tensor.matmul(ss[i][:, :w], ident[:], hy2[:, :w], start=True, stop=False)
+            nc.tensor.matmul(ss[i][:, :w], ident[:], hx2[:, :w], start=False, stop=True)
+
+        def ln(i):
+            h, g, t, ui, m0, m1 = tiles[i]
+            w = m1 - m0
+            if ui not in E:
+                E[ui] = work.tile([P, 4, H], F32, name="e", tag="e", bufs=3, align_bytes=64)
+            nc.scalar.activation(out=E[ui][:, t, m0:m1], in_=ss[i][:, :w], func=ACT.Ln, scale=col(2, g, t), bias=1.0)
+
+        def exp(ui, m0, m1):
+            nc.scalar.activation(out=E[ui][:, :, m0:m1], in_=E[ui][:, :, m0:m1], func=ACT.Exp, scale=-0.3)
+
+        def flux(ui, a, m0, m1):
+            d = FX if a == 0 else FY
+            src = gX if a == 0 else gY
+            if ui not in d:
+                d[ui] = work.tile([P, H, 4], BF16, name="f" + str(a), tag="f" + str(a), bufs=2, align_bytes=64)
+            nc.vector.scalar_tensor_tensor(
+                out=d[ui][:, m0:m1, :], in0=E[ui][:, :, m0:m1].rearrange("p t m -> p m t"), scalar=1.0 / 9.0,
+                in1=src[ui][:, :, m0:m1].rearrange("p t m -> p m t"), op0=ALU.add, op1=ALU.mult)
+
+        def fquant(ui, a, m0, m1):
+            d = FX if a == 0 else FY
+            if (ui, a) not in fq:
+                c = work.tile([P, H], U32, name="fc" + str(a), tag="fc" + str(a), bufs=4, align_bytes=64)
+                s = work.tile([P, H], U8, name="fs" + str(a), tag="fs" + str(a), bufs=4, align_bytes=64)
+                fq[(ui, a)] = (c, s)
+            c, s = fq[(ui, a)]
+            nc.vector.quantize_mx(out=c[:, m0:m1].bitcast(FP8X4), scales=s[:, m0:m1],
+                                  in_=d[ui][:, m0:m1, :].rearrange("p m t -> p (m t)"))
+
+        def stage2(acc, ui, j, start, stop):
+            h, g = UNITS[ui]
+            for a in range(2):
+                c, s = fq[(ui, a)]
+                nc.tensor.matmul_mx(
+                    out=acc[:], lhsT=c[:, j * P:(j + 1) * P].bitcast(FP8X4), lhsT_scale=s[:, j * P:(j + 1) * P],
+                    rhs=pw[:, a, g, :].bitcast(FP4X4), rhs_scale=psc[:, a, g, :],
+                    start=(start and a == 0), stop=(stop and a == 1))
+
+        def evac(acc, h, j):
+            o = work.tile([P, R], F32, name="o", tag="o", bufs=3, align_bytes=64)
+            nc.vector.tensor_tensor(out=o[:], in0=acc[:], in1=load_bc[:], op=ALU.subtract)
+            nc.sync.dma_start(out=out[h * H + j * P:h * H + (j + 1) * P, :], in_=o[:])
+
+        HEADTAGS = [["px", "py"], ["ss", "acc"]]
+        for r in range(4):
+            product(0, r)
+            transposes(0, r, HEADTAGS[r // 2])
+            if r % 2 == 1:
+                for g in range(KG):
+                    tcopy(0, r // 2, g, scopy)
+            if r == 1:
+                vps = psum.tile([P, 4, P], BF16, name="vps", tag="ss", bufs=BANKS["ss"])
+                for t in range(4):
+                    nc.tensor.transpose(vps[:, t, :], vrow[:, t::4], identb[:])
+                perm_words(0, 0)
+                perm_scales(0)
+                nc.vector.tensor_copy(out=vecs[:], in_=vps[:, :, 0:21])
+                if SPLIT:
+                    uquant(0, 0, 0, 256)
+                    uquant(0, 1, 0, 256)
+        nc.gpsimd.tensor_scalar(out=k9[:], in0=vecs[:, :, 9:21], scalar1=0.9, scalar2=0.0, op0=ALU.mult, op1=ALU.add)
+        for a in range(2):
+            nc.gpsimd.tensor_tensor(out=cc[:, :, 3 * a:3 * a + 3], in0=k9[:, :, 6 * a:6 * a + 3], in1=vecs[:, :, 0:3], op=ALU.mult)
+            nc.gpsimd.tensor_tensor(out=cm[:, :, 3 * a:3 * a + 3], in0=k9[:, :, 6 * a + 3:6 * a + 6], in1=vecs[:, :, 3:6], op=ALU.mult)
+        nc.gpsimd.tensor_tensor(out=cc[:], in0=cc[:], in1=cm[:], op=ALU.add)
+        if SPLIT:
+            stage1(0)
+            uquant(0, 0, 256, H)
+            uquant(0, 1, 256, H)
+        else:
+            uquant(0, 0, 0, H)
+            uquant(0, 1, 0, H)
+        perm_words(0, 1)
+        late_loads()
+        if not SPLIT:
+            stage1(0)
+
+        extra = {i: [] for i in range(NT + 3)}
+        for g in range(QG):
+            for t in range(4):
+                i0 = [n for n in range(NT) if tiles[n][1] == g and tiles[n][2] == t][0]
+                if (g, t) > (0, 1):
+                    extra[max(0, i0 - 2)].append(lambda g=g, t=t: perm_words(g, t))
+        extra[PS[0]].append(lambda: perm_scales(1))
+        extra[PS[1]].append(lambda: perm_scales(2))
+
+        pre = {i: [] for i in range(NT + 3)}
+
+        def turn(rp, g):
+            for r in (2 * rp, 2 * rp + 1):
+                words = ubf[(1, r)][:].bitcast(F32)
+                if r % 2 == 0:
+                    tp[(1, rp, g)] = bank("acc")
+                for w in range(2):
+                    c0 = (r % 2) * 256 + w * 128
+                    nc.tensor.transpose(tp[(1, rp, g)][:, c0:c0 + 128], words[:, 256 * g + w:256 * (g + 1):2], ident[:])
+
+        for r in range(4):
+            extra[UPREP[r]].append(lambda r=r: product(1, r))
+        for n in range(4):
+            pre[UPT[n]].append(lambda n=n: turn(n // 2, n % 2))
+            extra[UPT[n]].append(lambda n=n: tcopy(1, n // 2, n % 2, scopy))
+            if n >= 2:
+                extra[UPT[n] + 1].append(lambda n=n: uquant(1, n % 2, 0, H))
+
+        def phase2(parts):
+            work_list, prev = [], []
+            for ui, m0, m1 in parts:
+                for a in range(2):
+                    for c in range(m0, m1, 256):
+                        work_list.append(lambda ui=ui, a=a, c=c: flux(ui, a, c, c + 256))
+                    work_list.extend(prev)
+                    prev = [lambda ui=ui, a=a, m0=m0, m1=m1: fquant(ui, a, m0, m1)]
+            work_list.extend(prev)
+            return work_list
+
+        accs = {}
+
+        def out_h0(j):
+            accs[j] = bank("acc")
+            for ui in range(3):
+                stage2(accs[j], ui, j, ui == 0, ui == 2)
+
+        def spread(items, s0, s1):
+            for n, f in enumerate(items):
+                extra[min(NT + GLAG - 1, s0 + int(n * (s1 - s0) / len(items)))].append(f)
+
+        ends = sorted(batch_end)
+        for bi in range(len(ends) - 1):
+            w1 = phase2(BATCHES[bi])
+            c0, c1 = ends[bi] + 1, ends[bi + 1] + 1
+            n0 = int(len(w1) * BURST[bi])
+            extra[c0].extend(w1[:n0])
+            spread(w1[n0:], c0 + 1, c1 + LAG2[bi])
+        for j in range(4):
+            extra[first_h1 + OUTS[j]].append(lambda j=j: out_h0(j))
+            extra[min(NT + 1, first_h1 + OUTS[j] + 1)].append(lambda j=j: evac(accs[j], 0, j))
+
+        lnq, expq = [], []
+
+        def finish(i):
+            if i == last:
+                while expq:
+                    exp(*expq.pop(0))
+            if i >= 0:
+                lnq.append(i)
+            if not expq:
+                while lnq:
+                    n = lnq.pop(0)
+                    ln(n)
+                    if n in batch_end and n != last:
+                        for ui, m0, m1 in batch_end[n]:
+                            for c in range(m0, m1, 256):
+                                expq.append((ui, c, c + 256))
+                        break
+            for n in range(min(len(expq), EXPS)):
+                exp(*expq.pop(0))
+
+        for i in range(NT + max(GLAG, LNLAG)):
+            for f in pre[i]:
+                f()
+            if i < last:
+                stage1(i + 1)
+            if i < NT:
+                squares(i)
+                if MODE[i] in ("S", "V"):
+                    t1(i)
+                if i not in SADD_ON_V:
+                    sadd(i)
+                if MODE[i] == "S":
+                    t2(i, False)
+            if LNLAG <= i <= NT - 1 + LNLAG:
+                finish(i - LNLAG)
+            ex = extra[i]
+            cut = int(len(ex) * 1)
+            if GLAG and 0 < i <= NT:
+                gradients(i - 1)
+            for f in ex[:cut]:
+                f()
+            if i < NT and MODE[i] == "V":
+                t2(i, True)
+            if i < NT and i in SADD_ON_V:
+                sadd(i)
+            if not GLAG and i < NT:
+                gradients(i)
+            for f in ex[cut:]:
+                f()
+        for i in range(NT + max(GLAG, LNLAG), NT + 3):
+            for f in extra[i]:
+                f()
+
+        final = BATCHES[-1][0][1] // P
+        tail = {}
+        for j, tag in ((0, "acc"), (1, "ss"), (2, "px"), (3, "py")):
+            if j >= final:
+                tail[j] = bank(tag)
+                stage2(tail[j], 3, j, True, False)
+                stage2(tail[j], 4, j, False, False)
+                exp(5, j * P, (j + 1) * P)
+            else:
+                tail[j] = bank(tag)
+                for ui in (3, 4, 5):
+                    stage2(tail[j], ui, j, ui == 3, ui == 5)
+        for j in range(final, 4):
+            m = (j * P, (j + 1) * P)
+            flux(5, 0, m[0], m[1])
+            flux(5, 1, m[0], m[1])
+            if j == final:
+                for jj in range(final):
+                    evac(tail[jj], 1, jj)
+            fquant(5, 0, m[0], m[1])
+            fquant(5, 1, m[0], m[1])
+            stage2(tail[j], 5, j, False, True)
+            if j > final:
+                evac(tail[j - 1], 1, j - 1)
+        evac(tail[3], 1, 3)

@@ -36,6 +36,7 @@ UPT = [5, 6, 8, 9]
 SPLIT = 0
 GLAG = 1
 LNLAG = 1
+ETA = "VVVVVV"
 
 
 def tile_carreau_galerkin_residual_f1_kernel(
@@ -269,17 +270,37 @@ def tile_carreau_galerkin_residual_f1_kernel(
                 E[ui] = work.tile([P, 4, H], F32, name="e", tag="e", bufs=3, align_bytes=64)
             nc.scalar.activation(out=E[ui][:, t, m0:m1], in_=ss[i][:, :w], func=ACT.Ln, scale=col(2, g, t), bias=1.0)
 
+        state = {}
+
         def exp(ui, m0, m1):
+            for c in range(m0, m1, P):
+                assert state.get((ui, c)) is None
+                state[(ui, c)] = 1
             nc.scalar.activation(out=E[ui][:, :, m0:m1], in_=E[ui][:, :, m0:m1], func=ACT.Exp, scale=-0.3)
+
+        def eta(ui, m0, m1):
+            e = E[ui][:, :, m0:m1]
+            for c in range(m0, m1, P):
+                assert state.get((ui, c)) == 1
+                state[(ui, c)] = 2
+            if ETA[ui] == "V":
+                nc.vector.tensor_scalar_add(out=e, in0=e, scalar1=1.0 / 9.0)
+            elif ETA[ui] == "S":
+                nc.scalar.activation(out=e, in_=e, func=ACT.Copy, bias=1.0 / 9.0)
+            else:
+                nc.gpsimd.tensor_scalar(out=e, in0=e, scalar1=1.0, scalar2=1.0 / 9.0, op0=ALU.mult, op1=ALU.add)
 
         def flux(ui, a, m0, m1):
             d = FX if a == 0 else FY
             src = gX if a == 0 else gY
+            for c in range(m0, m1, P):
+                assert state.get((ui, c)) == 2
             if ui not in d:
                 d[ui] = work.tile([P, H, 4], BF16, name="f" + str(a), tag="f" + str(a), bufs=2, align_bytes=64)
-            nc.vector.scalar_tensor_tensor(
-                out=d[ui][:, m0:m1, :], in0=E[ui][:, :, m0:m1].rearrange("p t m -> p m t"), scalar=1.0 / 9.0,
-                in1=src[ui][:, :, m0:m1].rearrange("p t m -> p m t"), op0=ALU.add, op1=ALU.mult)
+            nc.vector.tensor_tensor(
+                out=d[ui][:, m0:m1, :].rearrange("p (c i) t -> p c t i", i=4),
+                in0=E[ui][:, :, m0:m1].rearrange("p t (c i) -> p c t i", i=4),
+                in1=src[ui][:, :, m0:m1].rearrange("p t (c i) -> p c t i", i=4), op=ALU.mult)
 
         def fquant(ui, a, m0, m1):
             d = FX if a == 0 else FY
@@ -370,6 +391,9 @@ def tile_carreau_galerkin_residual_f1_kernel(
         def phase2(parts):
             work_list, prev = [], []
             for ui, m0, m1 in parts:
+                if ETA[ui] == "V":
+                    for c in range(m0, m1, 256):
+                        work_list.append(lambda ui=ui, c=c: eta(ui, c, c + 256))
                 for a in range(2):
                     for c in range(m0, m1, 256):
                         work_list.append(lambda ui=ui, a=a, c=c: flux(ui, a, c, c + 256))
@@ -405,7 +429,10 @@ def tile_carreau_galerkin_residual_f1_kernel(
         def finish(i):
             if i == last:
                 while expq:
-                    exp(*expq.pop(0))
+                    e = expq.pop(0)
+                    exp(*e)
+                    if ETA[e[0]] != "V":
+                        eta(*e)
             if i >= 0:
                 lnq.append(i)
             if not expq:
@@ -418,7 +445,10 @@ def tile_carreau_galerkin_residual_f1_kernel(
                                 expq.append((ui, c, c + 256))
                         break
             for n in range(min(len(expq), EXPS)):
-                exp(*expq.pop(0))
+                e = expq.pop(0)
+                exp(*e)
+                if ETA[e[0]] != "V":
+                    eta(*e)
 
         for i in range(NT + max(GLAG, LNLAG)):
             for f in pre[i]:
@@ -461,12 +491,16 @@ def tile_carreau_galerkin_residual_f1_kernel(
                 stage2(tail[j], 3, j, True, False)
                 stage2(tail[j], 4, j, False, False)
                 exp(5, j * P, (j + 1) * P)
+                if ETA[5] != "V":
+                    eta(5, j * P, (j + 1) * P)
             else:
                 tail[j] = bank(tag)
                 for ui in (3, 4, 5):
                     stage2(tail[j], ui, j, ui == 3, ui == 5)
         for j in range(final, 4):
             m = (j * P, (j + 1) * P)
+            if ETA[5] == "V":
+                eta(5, m[0], m[1])
             flux(5, 0, m[0], m[1])
             flux(5, 1, m[0], m[1])
             if j == final:

from contextlib import ExitStack

import concourse.mybir as mybir
from concourse.masks import make_identity

M, K, Q, R = 1024, 1024, 1536, 512
FLOPS = 2 * M * K * 2 * Q + 2 * M * Q * 2 * R

F32 = mybir.dt.float32
BF16 = mybir.dt.bfloat16
I32 = mybir.dt.int32
U32 = mybir.dt.uint32
U8 = mybir.dt.uint8
FP8 = mybir.dt.float8_e4m3fn
FP8X4 = mybir.dt.float8_e4m3fn_x4
FP4X4 = mybir.dt.float4_e2m1fn_x4
ALU = mybir.AluOpType
ACT = mybir.ActivationFunctionType

P = 128
H = 512
KG = K // 512
QG = Q // 512
BANKS = {"px": 2, "py": 3, "ss": 2, "acc": 1}
UNITS = [(0, 0), (0, 1), (0, 2), (1, 0), (1, 1), (1, 2)]
BATCHES = [[(0, 0, 512), (1, 0, 512), (2, 0, 512)], [(3, 0, 512), (4, 0, 512)], [(5, 0, 512)]]
MODE = "GGGGGGGGGGGGGGGGGGGGGGGGGGGGGG"
SADD_ON_V = {1, 3, 5, 7, 9, 11, 13, 21}
EXPS = 2
BURST = [0, 0]
LAG2 = [0, 0]
OUTS = [7, 8, 9, 10]
UPREP = [2, 3, 6, 7]
PS = [1, 5]
UPT = [5, 6, 8, 9]
SPLIT = 0
GLAG = 1
LNLAG = 1
ETA = "VVVVVV"


def tile_carreau_galerkin_residual_f1_kernel(
    tc, u_bytes, u_scale, bx_words, bx_scales, by_words, by_scales, lift_x, lift_y, lam,
    kxx, kxy, kyx, kyy, px_words, px_scales, py_words, py_scales, load, out
):
    nc = tc.nc
    with ExitStack() as ctx:
        keep = ctx.enter_context(tc.tile_pool(name="keep", bufs=1))
        work = ctx.enter_context(tc.tile_pool(name="work", bufs=2))
        psum = ctx.enter_context(tc.psum_pool(name="psum", bufs=2))
        ctx.enter_context(tc.manual_schedule(engines={mybir.EngineType.Activation}))

        scale_bc = keep.tile([P, K], F32, name="scale_bc", align_bytes=64)
        load_bc = keep.tile([P, R], BF16, name="load_bc", align_bytes=64)
        uq = keep.tile([P, KG, M], U32, name="uq", align_bytes=64)
        uqs = keep.tile([P, KG, M], U8, name="uqs", align_bytes=64)
        raws = keep.tile([P, 2, KG, Q], U8, name="raws", align_bytes=64)
        perms = keep.tile([P, QG, 2 * KG, 4, P], U8, name="perms", align_bytes=64)
        permw = keep.tile([P, QG, 4, 2 * KG, 2 * P], U8, name="permw", align_bytes=64)
        pw = keep.tile([P, 2, QG, 2 * R], U8, name="pw", align_bytes=64)
        psc = keep.tile([P, 2, QG, R], U8, name="psc", align_bytes=64)
        vrow = keep.tile([P, 512], BF16, name="vrow", align_bytes=64)
        vecs = keep.tile([P, 4, 21], F32, name="vecs", align_bytes=64)
        k9 = keep.tile([P, 4, 12], F32, name="k9", align_bytes=64)
        cc = keep.tile([P, 4, 6], F32, name="cc", align_bytes=64)
        cm = keep.tile([P, 4, 6], F32, name="cm", align_bytes=64)
        dummy = keep.tile([P, 2], F32, name="dummy", align_bytes=64)
        ident = keep.tile([P, P], F32, name="ident", align_bytes=64)
        identb = keep.tile([P, P], BF16, name="identb", align_bytes=64)

        ub = []
        for h in range(2):
            ubh = work.tile([P, 4, K], U8, name="ubh", tag="ubh", bufs=2, align_bytes=64)
            ub.append(ubh)
        rawws = []
        nc.vector.memset(raws[:].rearrange("p a k n -> p (a k n)").bitcast(I32), 0)
        nc.sync.dma_start(out=scale_bc[:], in_=u_scale.rearrange("o k -> (o k)").partition_broadcast(P))
        for r in range(4):
            nc.sync.dma_start(out=ub[0][:, r, :], in_=u_bytes[r * P:(r + 1) * P, :])

        def load_raww(g):
            rw = work.tile([P, 2, KG, 1024], U8, name="rw", tag="rw", bufs=2, align_bytes=64)
            for a, w in ((0, bx_words), (1, by_words)):
                nc.sync.dma_start(out=rw[:, a, :, :], in_=w[:, :, g * 1024:(g + 1) * 1024].rearrange("k p c -> p k c"))
            rawws.append(rw)

        for a, s in ((0, bx_scales), (1, by_scales)):
            for q4 in range(4):
                nc.sync.dma_start(
                    out=raws[32 * q4:32 * q4 + 4, a, :, :].bitcast(I32),
                    in_=s[:, 4 * q4:4 * q4 + 4, :].rearrange("k r n -> r k n").bitcast(I32))
        load_raww(0)
        nc.gpsimd.memset(vrow[:], 0.0)
        nc.gpsimd.memset(dummy[:], 1.0)
        make_identity(nc, ident[:])
        make_identity(nc, identb[:])
        nc.gpsimd.memset(psc[:].rearrange("p a g n -> p (a g n)").bitcast(I32), 0)
        for v, vec in enumerate((lift_x, lift_y, lam, kxx, kxy, kyx, kyy)):
            nc.scalar.dma_start(out=vrow[3 * v:3 * v + 3, :], in_=vec.rearrange("(g n) -> g n", g=QG))
        nc.scalar.activation(out=dummy[:, 1:2], in_=dummy[:, 0:1], func=ACT.Ln)
        nc.sync.dma_start(out=ub[1][:], in_=u_bytes[H:2 * H, :].rearrange("(r p) k -> p r k", p=P))
        load_raww(1)
        nc.scalar.dma_start(out=load_bc[:], in_=load.partition_broadcast(P))

        def late_loads():
            load_raww(2)
            for a, w in ((0, px_words), (1, py_words)):
                nc.sync.dma_start(out=pw[:, a, :, :], in_=w.rearrange("g p c -> p g c"))
            for a, s in ((0, px_scales), (1, py_scales)):
                for q4 in range(4):
                    nc.sync.dma_start(
                        out=psc[32 * q4:32 * q4 + 4, a, :, :].bitcast(I32),
                        in_=s[:, 4 * q4:4 * q4 + 4, :].rearrange("g r n -> r g n").bitcast(I32))

        def bank(tag):
            t = psum.tile([P, 512], F32, name="ps_" + tag, tag=tag, bufs=BANKS[tag])
            return t

        ubf = {}
        uT = {}
        tp = {}

        def product(h, r):
            t = work.tile([P, K], BF16, name="ubf", tag="ubf", bufs=2, align_bytes=64)
            nc.vector.tensor_tensor(out=t[:], in0=ub[h][:, r, :].bitcast(FP8), in1=scale_bc[:], op=ALU.mult)
            ubf[(h, r)] = t

        def transposes(h, r, tags):
            words = ubf[(h, r)][:].bitcast(F32)
            for g in range(KG):
                if r % 2 == 0:
                    tp[(h, r // 2, g)] = bank(tags[g])
                b = tp[(h, r // 2, g)]
                for w in range(2):
                    c0 = (r % 2) * 256 + w * 128
                    nc.tensor.transpose(b[:, c0:c0 + 128], words[:, 256 * g + w:256 * (g + 1):2], ident[:])

        def tcopy(h, rp, g, eng):
            if rp == 0:
                uT[(h, g)] = work.tile([P, 4 * H], BF16, name="uT", tag="uT", bufs=2, align_bytes=64)
            o = uT[(h, g)][:].bitcast(F32)[:, rp * 512:(rp + 1) * 512].rearrange("p (s n w) -> p s n w", s=2, w=2)
            i = tp[(h, rp, g)][:].rearrange("p (s w n) -> p s n w", s=2, w=2)
            eng(o, i)

        def scopy(o, i):
            nc.scalar.copy(out=o, in_=i)

        def vcopy(o, i):
            nc.vector.tensor_copy(out=o, in_=i)

        def uquant(h, g, m0, m1):
            n = slice(h * H + m0, h * H + m1)
            nc.vector.quantize_mx(out=uq[:, g, n].bitcast(FP8X4), scales=uqs[:, g, n],
                                  in_=uT[(h, g)][:, 4 * m0:4 * m1])

        def perm_scales(g):
            for a in range(2):
                nc.vector.tensor_copy(
                    out=perms[:, g, a * KG:(a + 1) * KG, :, :],
                    in_=raws[:, a, :, g * 512:(g + 1) * 512].rearrange("p k (m t) -> p k t m", t=4))

        def perm_words(g, t):
            nc.vector.tensor_copy(
                out=permw[:, g, t, :, :].rearrange("p k (m b) -> p k m b", b=2),
                in_=rawws[g][:].rearrange("p a k (m t b) -> p (a k) t m b", t=4, b=2)[:, :, t, :, :])

        tiles = []
        batch_end = {}
        for b in BATCHES:
            for ui, m0, m1 in b:
                h, g = UNITS[ui]
                for t in range(4):
                    ms = [(m0, m1)]
                    if ui == 0 and t < SPLIT:
                        ms = [(m0, 256), (256, m1)]
                    for a0, a1 in ms:
                        tiles.append((h, g, t, ui, a0, a1))
            batch_end[len(tiles) - 1] = b
        NT = len(tiles)
        last = NT - 1
        first_h1 = [n for n in range(NT) if tiles[n][0] == 1][0]
        px, py, ss, sq, tt = {}, {}, {}, {}, {}
        gX, gY, E, FX, FY = {}, {}, {}, {}, {}
        fq = {}

        def stage1(i):
            h, g, t, ui, m0, m1 = tiles[i]
            w = m1 - m0
            px[i], py[i] = bank("px"), bank("py")
            step = 512 if w == 512 else 128
            for a, b in ((1, py[i]), (0, px[i])):
                for c in range(0, w, step):
                    n0 = h * H + m0 + c
                    for k in range(KG):
                        nc.tensor.matmul_mx(
                            out=b[:, c:c + step], lhsT=permw[:, g, t, a * KG + k, :].bitcast(FP4X4),
                            lhsT_scale=perms[:, g, a * KG + k, t, :],
                            rhs=uq[:, k, n0:n0 + step].bitcast(FP8X4),
                            rhs_scale=uqs[:, k, n0:n0 + step], start=(k == 0), stop=(k == KG - 1))

        def col(v, g, t):
            return vecs[:, t, 3 * v + g:3 * v + g + 1]

        def squares(i):
            h, g, t, ui, m0, m1 = tiles[i]
            w = m1 - m0
            hy2 = work.tile([P, H], F32, name="hy2", tag="hy2", bufs=2, align_bytes=64)
            nc.scalar.activation(out=hy2[:, :w], in_=py[i][:, :w], func=ACT.Square, bias=col(1, g, t))
            hx2 = work.tile([P, H], F32, name="hx2", tag="hx2", bufs=2, align_bytes=64)
            if MODE[i] == "G":
                hx = work.tile([P, H], F32, name="hx", tag="hx", bufs=2, align_bytes=64)
                nc.scalar.activation(out=hx[:, :w], in_=px[i][:, :w], func=ACT.Identity, bias=col(0, g, t))
                nc.scalar.activation(out=hx2[:, :w], in_=hx[:, :w], func=ACT.Square)
                for a in range(2):
                    tx = work.tile([P, H], F32, name="t" + "xy"[a], tag="t" + "xy"[a], bufs=2, align_bytes=64)
                    nc.gpsimd.tensor_scalar(out=tx[:, :w], in0=hx[:, :w], scalar1=k9[:, t, 6 * a + g:6 * a + g + 1],
                                            scalar2=cm[:, t, 3 * a + g:3 * a + g + 1], op0=ALU.mult, op1=ALU.add)
                    tt[(i, a)] = tx
            else:
                nc.scalar.activation(out=hx2[:, :w], in_=px[i][:, :w], func=ACT.Square, bias=col(0, g, t))
            sq[i] = (hx2, hy2)

        def t1(i):
            h, g, t, ui, m0, m1 = tiles[i]
            w = m1 - m0
            tx = work.tile([P, H], F32, name="tx", tag="tx", bufs=2, align_bytes=64)
            nc.scalar.activation(out=tx[:, :w], in_=px[i][:, :w], func=ACT.Identity, scale=k9[:, t, g:g + 1], bias=cc[:, t, g:g + 1])
            tt[(i, 0)] = tx

        def t2(i, on_v):
            h, g, t, ui, m0, m1 = tiles[i]
            w = m1 - m0
            ty = work.tile([P, H], F32, name="ty", tag="ty", bufs=2, align_bytes=64)
            if on_v:
                nc.vector.tensor_scalar(out=ty[:, :w], in0=px[i][:, :w], scalar1=k9[:, t, 6 + g:7 + g],
                                        scalar2=cc[:, t, 3 + g:4 + g], op0=ALU.mult, op1=ALU.add)
            else:
                nc.scalar.activation(out=ty[:, :w], in_=px[i][:, :w], func=ACT.Identity, scale=k9[:, t, 6 + g:7 + g],
                                     bias=cc[:, t, 3 + g:4 + g])
            tt[(i, 1)] = ty

        def gradients(i):
            h, g, t, ui, m0, m1 = tiles[i]
            w = m1 - m0
            if ui not in gX:
                gX[ui] = work.tile([P, 4, H], F32, name="gx", tag="gx", bufs=4, align_bytes=64)
                gY[ui] = work.tile([P, 4, H], F32, name="gy", tag="gy", bufs=4, align_bytes=64)
            for a, dst in ((0, gX[ui]), (1, gY[ui])):
                kc = 3 + g if a == 0 else 9 + g
                nc.vector.scalar_tensor_tensor(out=dst[:, t, m0:m1], in0=py[i][:, :w], scalar=k9[:, t, kc:kc + 1],
                                               in1=tt[(i, a)][:, :w], op0=ALU.mult, op1=ALU.add)

        def sadd(i):
            h, g, t, ui, m0, m1 = tiles[i]
            w = m1 - m0
            hx2, hy2 = sq[i]
            if i in SADD_ON_V:
                sv = work.tile([P, H], F32, name="sv", tag="sv", bufs=3, align_bytes=64)
                ss[i] = sv
                nc.vector.tensor_tensor(out=sv[:, :w], in0=hx2[:, :w], in1=hy2[:, :w], op=ALU.add)
                return
            ss[i] = bank("ss")
            nc.tensor.matmul(ss[i][:, :w], ident[:], hy2[:, :w], start=True, stop=False)
            nc.tensor.matmul(ss[i][:, :w], ident[:], hx2[:, :w], start=False, stop=True)

        def ln(i):
            h, g, t, ui, m0, m1 = tiles[i]
            w = m1 - m0
            if ui not in E:
                E[ui] = work.tile([P, 4, H], F32, name="e", tag="e", bufs=3, align_bytes=64)
            nc.scalar.activation(out=E[ui][:, t, m0:m1], in_=ss[i][:, :w], func=ACT.Ln, scale=col(2, g, t), bias=1.0)

        state = {}

        def exp(ui, m0, m1):
            for c in range(m0, m1, P):
                assert state.get((ui, c)) is None
                state[(ui, c)] = 1
            nc.scalar.activation(out=E[ui][:, :, m0:m1], in_=E[ui][:, :, m0:m1], func=ACT.Exp, scale=-0.3)

        def eta(ui, m0, m1):
            e = E[ui][:, :, m0:m1]
            for c in range(m0, m1, P):
                assert state.get((ui, c)) == 1
                state[(ui, c)] = 2
            if ETA[ui] == "V":
                nc.vector.tensor_scalar_add(out=e, in0=e, scalar1=1.0 / 9.0)
            elif ETA[ui] == "S":
                nc.scalar.activation(out=e, in_=e, func=ACT.Copy, bias=1.0 / 9.0)
            else:
                nc.gpsimd.tensor_scalar(out=e, in0=e, scalar1=1.0, scalar2=1.0 / 9.0, op0=ALU.mult, op1=ALU.add)

        def flux(ui, a, m0, m1):
            d = FX if a == 0 else FY
            src = gX if a == 0 else gY
            for c in range(m0, m1, P):
                assert state.get((ui, c)) == 2
            if ui not in d:
                d[ui] = work.tile([P, H, 4], BF16, name="f" + str(a), tag="f" + str(a), bufs=2, align_bytes=64)
            nc.vector.tensor_tensor(
                out=d[ui][:, m0:m1, :].rearrange("p (c i) t -> p c t i", i=4),
                in0=E[ui][:, :, m0:m1].rearrange("p t (c i) -> p c t i", i=4),
                in1=src[ui][:, :, m0:m1].rearrange("p t (c i) -> p c t i", i=4), op=ALU.mult)

        def fquant(ui, a, m0, m1):
            d = FX if a == 0 else FY
            if (ui, a) not in fq:
                c = work.tile([P, H], U32, name="fc" + str(a), tag="fc" + str(a), bufs=4, align_bytes=64)
                s = work.tile([P, H], U8, name="fs" + str(a), tag="fs" + str(a), bufs=4, align_bytes=64)
                fq[(ui, a)] = (c, s)
            c, s = fq[(ui, a)]
            nc.vector.quantize_mx(out=c[:, m0:m1].bitcast(FP8X4), scales=s[:, m0:m1],
                                  in_=d[ui][:, m0:m1, :].rearrange("p m t -> p (m t)"))

        def stage2(acc, ui, j, start, stop):
            h, g = UNITS[ui]
            for a in range(2):
                c, s = fq[(ui, a)]
                nc.tensor.matmul_mx(
                    out=acc[:], lhsT=c[:, j * P:(j + 1) * P].bitcast(FP8X4), lhsT_scale=s[:, j * P:(j + 1) * P],
                    rhs=pw[:, a, g, :].bitcast(FP4X4), rhs_scale=psc[:, a, g, :],
                    start=(start and a == 0), stop=(stop and a == 1))

        def evac(acc, h, j):
            o = work.tile([P, R], F32, name="o", tag="o", bufs=3, align_bytes=64)
            nc.vector.tensor_tensor(out=o[:], in0=acc[:], in1=load_bc[:], op=ALU.subtract)
            nc.sync.dma_start(out=out[h * H + j * P:h * H + (j + 1) * P, :], in_=o[:])

        HEADTAGS = [["px", "py"], ["ss", "acc"]]
        for r in range(4):
            product(0, r)
            transposes(0, r, HEADTAGS[r // 2])
            if r % 2 == 1:
                for g in range(KG):
                    tcopy(0, r // 2, g, scopy)
            if r == 1:
                vps = psum.tile([P, 4, P], BF16, name="vps", tag="ss", bufs=BANKS["ss"])
                for t in range(4):
                    nc.tensor.transpose(vps[:, t, :], vrow[:, t::4], identb[:])
                perm_words(0, 0)
                perm_scales(0)
                nc.vector.tensor_copy(out=vecs[:], in_=vps[:, :, 0:21])
                if SPLIT:
                    uquant(0, 0, 0, 256)
                    uquant(0, 1, 0, 256)
        nc.gpsimd.tensor_scalar(out=k9[:], in0=vecs[:, :, 9:21], scalar1=0.9, scalar2=0.0, op0=ALU.mult, op1=ALU.add)
        for a in range(2):
            nc.gpsimd.tensor_tensor(out=cc[:, :, 3 * a:3 * a + 3], in0=k9[:, :, 6 * a:6 * a + 3], in1=vecs[:, :, 0:3], op=ALU.mult)
            nc.gpsimd.tensor_tensor(out=cm[:, :, 3 * a:3 * a + 3], in0=k9[:, :, 6 * a + 3:6 * a + 6], in1=vecs[:, :, 3:6], op=ALU.mult)
        nc.gpsimd.tensor_tensor(out=cc[:], in0=cc[:], in1=cm[:], op=ALU.add)
        if SPLIT:
            stage1(0)
            uquant(0, 0, 256, H)
            uquant(0, 1, 256, H)
        else:
            uquant(0, 0, 0, H)
            uquant(0, 1, 0, H)
        perm_words(0, 1)
        late_loads()
        if not SPLIT:
            stage1(0)

        extra = {i: [] for i in range(NT + 3)}
        for g in range(QG):
            for t in range(4):
                i0 = [n for n in range(NT) if tiles[n][1] == g and tiles[n][2] == t][0]
                if (g, t) > (0, 1):
                    extra[max(0, i0 - 2)].append(lambda g=g, t=t: perm_words(g, t))
        extra[PS[0]].append(lambda: perm_scales(1))
        extra[PS[1]].append(lambda: perm_scales(2))

        pre = {i: [] for i in range(NT + 3)}

        def turn(rp, g):
            for r in (2 * rp, 2 * rp + 1):
                words = ubf[(1, r)][:].bitcast(F32)
                if r % 2 == 0:
                    tp[(1, rp, g)] = bank("acc")
                for w in range(2):
                    c0 = (r % 2) * 256 + w * 128
                    nc.tensor.transpose(tp[(1, rp, g)][:, c0:c0 + 128], words[:, 256 * g + w:256 * (g + 1):2], ident[:])

        for r in range(4):
            extra[UPREP[r]].append(lambda r=r: product(1, r))
        for n in range(4):
            pre[UPT[n]].append(lambda n=n: turn(n // 2, n % 2))
            extra[UPT[n]].append(lambda n=n: tcopy(1, n // 2, n % 2, scopy))
            if n >= 2:
                extra[UPT[n] + 1].append(lambda n=n: uquant(1, n % 2, 0, H))

        def phase2(parts):
            work_list, prev = [], []
            for ui, m0, m1 in parts:
                if ETA[ui] == "V":
                    for c in range(m0, m1, 256):
                        work_list.append(lambda ui=ui, c=c: eta(ui, c, c + 256))
                for a in range(2):
                    for c in range(m0, m1, 256):
                        work_list.append(lambda ui=ui, a=a, c=c: flux(ui, a, c, c + 256))
                    work_list.extend(prev)
                    prev = [lambda ui=ui, a=a, m0=m0, m1=m1: fquant(ui, a, m0, m1)]
            work_list.extend(prev)
            return work_list

        accs = {}

        def out_h0(j):
            accs[j] = bank("acc")
            for ui in range(3):
                stage2(accs[j], ui, j, ui == 0, ui == 2)

        def spread(items, s0, s1):
            for n, f in enumerate(items):
                extra[min(NT + GLAG - 1, s0 + int(n * (s1 - s0) / len(items)))].append(f)

        ends = sorted(batch_end)
        for bi in range(len(ends) - 1):
            w1 = phase2(BATCHES[bi])
            c0, c1 = ends[bi] + 1, ends[bi + 1] + 1
            n0 = int(len(w1) * BURST[bi])
            extra[c0].extend(w1[:n0])
            spread(w1[n0:], c0 + 1, c1 + LAG2[bi])
        for j in range(4):
            extra[first_h1 + OUTS[j]].append(lambda j=j: out_h0(j))
            extra[min(NT + 1, first_h1 + OUTS[j] + 1)].append(lambda j=j: evac(accs[j], 0, j))

        lnq, expq = [], []

        def finish(i):
            if i == last:
                while expq:
                    e = expq.pop(0)
                    exp(*e)
                    if ETA[e[0]] != "V":
                        eta(*e)
            if i >= 0:
                lnq.append(i)
            if not expq:
                while lnq:
                    n = lnq.pop(0)
                    ln(n)
                    if n in batch_end and n != last:
                        for ui, m0, m1 in batch_end[n]:
                            for c in range(m0, m1, 256):
                                expq.append((ui, c, c + 256))
                        break
            for n in range(min(len(expq), EXPS)):
                e = expq.pop(0)
                exp(*e)
                if ETA[e[0]] != "V":
                    eta(*e)

        for i in range(NT + max(GLAG, LNLAG)):
            for f in pre[i]:
                f()
            if i < last:
                stage1(i + 1)
            if i < NT:
                squares(i)
                if MODE[i] in ("S", "V"):
                    t1(i)
                if i not in SADD_ON_V:
                    sadd(i)
                if MODE[i] == "S":
                    t2(i, False)
            if LNLAG <= i <= NT - 1 + LNLAG:
                finish(i - LNLAG)
            ex = extra[i]
            cut = int(len(ex) * 1)
            if GLAG and 0 < i <= NT:
                gradients(i - 1)
            for f in ex[:cut]:
                f()
            if i < NT and MODE[i] == "V":
                t2(i, True)
            if i < NT and i in SADD_ON_V:
                sadd(i)
            if not GLAG and i < NT:
                gradients(i)
            for f in ex[cut:]:
                f()
        for i in range(NT + max(GLAG, LNLAG), NT + 3):
            for f in extra[i]:
                f()

        final = BATCHES[-1][0][1] // P
        tail = {}
        for j, tag in ((0, "acc"), (1, "ss"), (2, "px"), (3, "py")):
            if j >= final:
                tail[j] = bank(tag)
                stage2(tail[j], 3, j, True, False)
                stage2(tail[j], 4, j, False, False)
                exp(5, j * P, (j + 1) * P)
                if ETA[5] != "V":
                    eta(5, j * P, (j + 1) * P)
            else:
                tail[j] = bank(tag)
                for ui in (3, 4, 5):
                    stage2(tail[j], ui, j, ui == 3, ui == 5)
        for j in range(final, 4):
            m = (j * P, (j + 1) * P)
            if ETA[5] == "V":
                eta(5, m[0], m[1])
            flux(5, 0, m[0], m[1])
            flux(5, 1, m[0], m[1])
            if j == final:
                for jj in range(final):
                    evac(tail[jj], 1, jj)
            fquant(5, 0, m[0], m[1])
            fquant(5, 1, m[0], m[1])
            stage2(tail[j], 5, j, False, True)
            if j > final:
                evac(tail[j - 1], 1, j - 1)
        evac(tail[3], 1, 3)
